import numpy as np
import ml_dtypes


def mxq(x, axis, fmt="e4m3"):
    dtype, down = {"e4m3": (ml_dtypes.float8_e4m3fn, 7), "e5m2": (ml_dtypes.float8_e5m2, 14)}[fmt]
    v = np.moveaxis(np.asarray(x, np.float32).astype(ml_dtypes.bfloat16).astype(np.float64), axis, -1)
    blocks = v.reshape(v.shape[:-1] + (-1, 32))
    amax = np.abs(blocks).max(-1, keepdims=True)
    byte = np.maximum(np.where(amax > 0, np.frexp(amax)[1] - 1 + 127, 0) - down, 1)
    scale = np.exp2(byte - 127.0)
    codes = (blocks / scale).astype(np.float32).astype(dtype).astype(np.float64)
    return np.moveaxis((codes * scale).reshape(v.shape), -1, axis)


WIDE = False


def mx_kscale(k):
    if not WIDE:
        return np.ones(k)
    levels = np.array([10, -10, 5, -5, 0])
    if k % 512:
        return np.exp2(np.random.permutation(np.resize(levels, k // 32))).repeat(32)
    a = np.empty((k // 512, 16))
    for p in range(k // 512):
        a[p, :8] = np.random.permutation(np.resize(levels, 8))
        for g in range(8):
            far = levels[np.abs(levels - a[p, g]) >= 10]
            a[p, g + 8] = far[np.random.randint(len(far))]
    return np.exp2(a.ravel()).repeat(32)


def f64(x):
    return np.asarray(x).astype(np.float64)


def striped(idx):
    return np.tile(idx.reshape(-1, 16).T, (8, 1)).astype(np.uint16)


def unstriped(offs):
    return offs[:16].T.reshape(-1).astype(np.int64)


def striped8(idx):
    return np.concatenate([x.reshape(-1, 16).T for x in idx]).astype(np.uint16)


def runs(offs, k):
    lists = np.stack([offs[16 * r : 16 * r + 16].T.reshape(-1) for r in range(8)]).astype(np.int64)
    return lists[np.arange(k) % 512 // 64]


def pack_weight(w):
    k, n = w.shape
    w = f64(np.asarray(w, np.float32).astype(ml_dtypes.bfloat16)).reshape(k // 32, 32, n)
    amax = np.abs(w).max(1)
    byte = np.clip(np.where(amax > 0, np.frexp(amax)[1] - 1 + 127 - 7, 1), 1, 254)
    scaled = (w * np.exp2(127.0 - byte)[:, None, :]).reshape(k, n).astype(np.float32)
    words = np.ascontiguousarray(scaled.reshape(k // 512, 128, 4, n).transpose(0, 1, 3, 2)).astype(ml_dtypes.float8_e4m3fn).view(np.uint8)
    return words, np.ascontiguousarray(byte.astype(np.uint8).reshape(k // 512, 16, n))


def unpack_weight(words, scales):
    g, p, n, _ = words.shape
    vals = np.ascontiguousarray(words).view(ml_dtypes.float8_e4m3fn).astype(np.float64) * np.repeat(np.exp2(scales.astype(np.float64) - 127.0), 8, axis=1)[..., None]
    return vals.transpose(0, 1, 3, 2).reshape(g * 512, n)


E2M1 = np.array([0.0, 0.5, 1.0, 1.5, 2.0, 3.0, 4.0, 6.0, -0.0, -0.5, -1.0, -1.5, -2.0, -3.0, -4.0, -6.0])


def pack_fp4(w):
    k, n = w.shape
    w = f64(np.asarray(w, np.float32).astype(ml_dtypes.bfloat16)).reshape(k // 32, 32, n)
    amax = np.abs(w).max(1)
    mant, ex = np.frexp(amax / 6.0)
    byte = np.clip(np.where(amax > 0, np.where(mant > 0.5, ex, ex - 1) + 127, 1), 1, 254)
    scaled = (w * np.exp2(127.0 - byte)[:, None, :]).reshape(k, n).astype(np.float32)
    c = np.ascontiguousarray(scaled.reshape(k // 512, 128, 4, n).transpose(0, 1, 3, 2)).astype(ml_dtypes.float4_e2m1fn).view(np.uint8) & 0xF
    words = (c[..., 0::2] | (c[..., 1::2] << 4)).reshape(k // 512, 128, 2 * n)
    return np.ascontiguousarray(words), np.ascontiguousarray(byte.astype(np.uint8).reshape(k // 512, 16, n))


def unpack_fp4(words, scales):
    g, _, n = scales.shape
    words = np.ascontiguousarray(words).reshape(g, 128, n, 2)
    nib = np.empty((g, 128, n, 4), np.uint8)
    nib[..., 0::2] = words & 0xF
    nib[..., 1::2] = words >> 4
    vals = E2M1[nib] * np.repeat(np.exp2(scales.astype(np.float64) - 127.0), 8, axis=1)[..., None]
    return vals.transpose(0, 1, 3, 2).reshape(g * 512, n)


def relu(v):
    return np.maximum(v, 0.0)


def sigmoid(v):
    return 1.0 / (1.0 + np.exp(-np.maximum(v, -700.0)))


K, T, S, H, G, U = 512, 2048, 256, 512, 2048, 1024


def setup_inputs():
    n = np.random.standard_normal
    s = mx_kscale(K)[:, None]
    packed_xT = pack_weight(n((K, T)) * s)
    packed_w1 = pack_fp4(n((K, H)) / np.sqrt(K) / s)
    packed_dT = pack_weight(n((K, G)) / s)
    return {
        "x_words": packed_xT[0],
        "x_scales": packed_xT[1],
        "w1_words": packed_w1[0],
        "w1_scales": packed_w1[1],
        "sl": np.random.uniform(1.0, 2.0, (H, 1)).astype(np.float32),
        "th": (0.5 * n((H, 1))).astype(np.float32),
        "gs": (np.random.uniform(0.5, 1.5, (K, 1)) * s).astype(np.float32),
        "d_words": packed_dT[0],
        "d_scales": packed_dT[1],
        "offs": striped8(np.random.randint(0, T, (8, S))),
        "n1": striped(np.random.permutation(S)),
        "n2": striped(np.random.permutation(S)),
        "k1": striped8(np.random.randint(0, G, (8, H))),
        "n3": striped(np.random.permutation(U)[:S]),
        "n4": striped(np.random.permutation(S)),
    }


def reference(x_words, x_scales, w1_words, w1_scales, sl, th, gs, d_words, d_scales, offs, n1, n2, k1, n3, n4):
    d_k1 = unpack_weight(d_words, d_scales)[np.arange(K)[:, None], runs(k1, K)]
    xq = unpack_weight(x_words, x_scales)[np.arange(K)[:, None], runs(offs, K)]
    y = unpack_fp4(w1_words, w1_scales).T @ xq
    ds = np.zeros((H, S))
    ds[:, unstriped(n1)] = y
    sg = sigmoid(f64(sl) * (ds[:, unstriped(n2)] - f64(th)))
    z = f64(gs) * (y * sg)
    h = 0.0625 * ((d_k1.T @ mxq(z, 0, "e4m3")))
    nw = h - (relu(h[:, unstriped(n4)]))
    out = np.zeros((H, U))
    out[:, unstriped(n3)] = nw
    return out

@@ -1,0 +1,228 @@
+from contextlib import ExitStack
+
+import concourse.mybir as mybir
+
+K, T, S, H, G, U = 512, 2048, 256, 512, 2048, 1024
+FLOPS = 2 * K * H * S * 2
+
+F32 = mybir.dt.float32
+BF16 = mybir.dt.bfloat16
+I32 = mybir.dt.int32
+U32 = mybir.dt.uint32
+U16 = mybir.dt.uint16
+U8 = mybir.dt.uint8
+FP8X4 = mybir.dt.float8_e4m3fn_x4
+FP4X4 = mybir.dt.float4_e2m1fn_x4
+ALU = mybir.AluOpType
+ACT = mybir.ActivationFunctionType
+
+P = 128
+PACK = 4
+SHIFT = 14
+PLANE_ROWS = 100
+ALIGN = 64
+HALF = S // 2
+
+
+def load_scale_table(queue, table, scales):
+    rows = scales[0].bitcast(I32).rearrange("(a e) c -> e a c", e=2)
+    words = table[:].bitcast(I32)
+    for e in range(2):
+        queue.dma_start(out=words[e:P:2, :], in_=rows[e].unsqueeze(1).to_broadcast([8, 8, rows.shape[2]]))
+
+
+def tile_picked_hdenseerlpagez_none_p_kernel(
+    tc, x_words, x_scales, w1_words, w1_scales, sl, th, gs, d_words, d_scales, offs, n1, n2, k1, n3, n4, out
+):
+    nc = tc.nc
+    with ExitStack() as ctx:
+        lists = ctx.enter_context(tc.tile_pool(name="lists", bufs=1))
+        sb = ctx.enter_context(tc.tile_pool(name="sb", bufs=1))
+        words = ctx.enter_context(tc.tile_pool(name="words", bufs=1))
+        psum = ctx.enter_context(tc.psum_pool(name="psum", bufs=1))
+
+        def load_list(name, src):
+            tile = lists.tile(list(src.shape), U16, name=name)
+            nc.sync.dma_start(tile[:], src)
+            return tile
+
+        def tile(name, shape, dtype, tag=None):
+            return sb.tile(shape, dtype, name=name, tag=tag or name, align_bytes=ALIGN)
+
+        offs_t = load_list("offs_t", offs)
+        xs_table = tile("xs_table", [P, T], U8, tag="scale_table")
+        load_scale_table(nc.sync, xs_table, x_scales)
+
+        w1s_raw = tile("w1s_raw", [P, H], U8)
+        w1s_rows = w1_scales[0].bitcast(I32).rearrange("(q r) c -> r q c", r=4)
+        for r in range(4):
+            nc.sync.dma_start(
+                out=w1s_raw[:].bitcast(I32)[r:P:4, :], in_=w1s_rows[r].unsqueeze(1).to_broadcast([4, 8, H // 4])
+            )
+        w1w_raw = tile("w1w_raw", [P, 2 * H], U8)
+        nc.gpsimd.dma_start(out=w1w_raw[:].bitcast(I32), in_=w1_words[0].bitcast(I32))
+
+        xw_table = words.tile([P, T], I32, name="xw_table", align_bytes=ALIGN, offset=0)
+        nc.sync.dma_start(out=xw_table[:], in_=x_words[0].rearrange("p c r -> p (c r)").bitcast(I32))
+
+        n1_t = load_list("n1_t", n1)
+        sl_t = tile("sl_t", [P, PACK], F32)
+        th_t = tile("th_t", [P, PACK], F32)
+        gs_t = tile("gs_t", [P, PACK], F32)
+        nc.gpsimd.dma_start(out=sl_t[:], in_=sl.rearrange("(p t) o -> p (t o)", t=PACK))
+        nc.gpsimd.dma_start(out=th_t[:], in_=th.rearrange("(p t) o -> p (t o)", t=PACK))
+        sl_th = tile("sl_th", [P, PACK], F32)
+        bias_t = tile("bias_t", [P, PACK], F32)
+        nc.gpsimd.tensor_tensor(sl_th[:], sl_t[:], th_t[:], ALU.mult)
+        nc.gpsimd.tensor_scalar(bias_t[:], sl_th[:], -1.0, 0.0, ALU.mult, ALU.add)
+        n2_t = load_list("n2_t", n2)
+        k1_t = load_list("k1_t", k1)
+        nc.gpsimd.dma_start(out=gs_t[:], in_=gs.rearrange("(p t) o -> p (t o)", t=PACK))
+        n4_t = load_list("n4_t", n4)
+        n3_t = load_list("n3_t", n3)
+
+        x_plane = tile("x_plane", [P, S], U8, tag="page1")
+        d_plane = tile("d_plane", [P, H], U8)
+        nc.vector.memset(x_plane[:].bitcast(I32), 0)
+        nc.vector.memset(d_plane[:].bitcast(I32), 0)
+
+        xs_picked = tile("xs_picked", [P, S], U8)
+        nc.vector.tensor_copy(xs_picked[:], xs_table[:].indirect(offs_t[:]))
+        nc.sync.dma_start(
+            out=x_plane[:].bitcast(I32)[0:PLANE_ROWS, :], in_=xs_picked[:].bitcast(I32)[SHIFT : SHIFT + PLANE_ROWS, :]
+        )
+
+        w1_plane = tile("w1_plane", [P, H], U8, tag="page2")
+        nc.vector.tensor_copy(
+            w1_plane[:].rearrange("p (t m) -> p t m", t=PACK), w1s_raw[:].rearrange("p (m t) -> p t m", t=PACK)
+        )
+        w1_codes = tile("w1_codes", [P, 2 * H], U8, tag="page3")
+        nc.scalar.copy(
+            w1_codes[:].bitcast(U16).rearrange("p (t m) -> p t m", t=PACK),
+            w1w_raw[:].bitcast(U16).rearrange("p (m t) -> p t m", t=PACK),
+        )
+        x_codes = tile("x_codes", [P, S], U32, tag="bytes")
+        nc.vector.tensor_copy(x_codes[:], xw_table[:].bitcast(U32).indirect(offs_t[:]))
+
+        y_ps, y_sb = [], []
+        for t in range(PACK):
+            acc = psum.tile([P, S], F32, name=f"y_ps{t}")
+            nc.tensor.matmul_mx(
+                out=acc[:],
+                lhsT=w1_codes[:, 2 * P * t : 2 * P * (t + 1)].bitcast(FP4X4),
+                lhsT_scale=w1_plane[:, P * t : P * (t + 1)],
+                rhs=x_codes[:].bitcast(FP8X4),
+                rhs_scale=x_plane[:],
+                start=True,
+                stop=True,
+            )
+            y_ps.append(acc)
+        for t in range(PACK):
+            y_sb.append(tile(f"y_sb{t}", [P, S], F32, tag="page0" if t == 0 else None))
+            nc.vector.tensor_copy(y_sb[t][:], y_ps[t][:])
+
+
+        ds_table = tile("ds_table", [P, G], U8, tag="scale_table")
+        load_scale_table(nc.sync, ds_table, d_scales)
+        dw_table = words.tile([P, G], I32, name="dw_table", align_bytes=ALIGN, offset=0)
+        nc.sync.dma_start(out=dw_table[:], in_=d_words[0].rearrange("p c r -> p (c r)").bitcast(I32))
+        ds_picked = tile("ds_picked", [P, H], U8, tag="bytes")
+        nc.vector.tensor_copy(ds_picked[:], ds_table[:].indirect(k1_t[:]))
+        nc.sync.dma_start(
+            out=d_plane[:].bitcast(I32)[0:PLANE_ROWS, :], in_=ds_picked[:].bitcast(I32)[SHIFT : SHIFT + PLANE_ROWS, :]
+        )
+        d_codes = tile("d_codes", [P, H], U32)
+        nc.vector.tensor_copy(d_codes[:], dw_table[:].bitcast(U32).indirect(k1_t[:]))
+
+        placed = [tile(f"placed{t}", [P, 2 * S], F32) for t in range(PACK)]
+        z_bf = [
+            words.tile([P, HALF, PACK], BF16, name=f"z_bf{a}", align_bytes=ALIGN, offset=a * HALF * PACK * 2)
+            for a in range(2)
+        ]
+        sg = [tile(f"sg{t}", [P, S], F32) for t in range(PACK)]
+
+        def place(t):
+            nc.scalar.activation(placed[t][:].indirect(n1_t[:]), y_sb[t][:], ACT.Copy)
+
+        def gate(t, lo, hi):
+            nc.scalar.activation(
+                sg[t][:, lo:hi],
+                placed[t][:].indirect(n2_t[:, lo // 16 : hi // 16]),
+                ACT.Sigmoid,
+                bias=bias_t[:, t : t + 1],
+                scale=sl_t[:, t : t + 1],
+            )
+            for a in range(lo // HALF, hi // HALF):
+                cols = slice(HALF * a, HALF * (a + 1))
+                nc.vector.scalar_tensor_tensor(
+                    z_bf[a][:, :, t], y_ps[t][:, cols], gs_t[:, t : t + 1], sg[t][:, cols], ALU.mult, ALU.mult
+                )
+
+        place(0)
+        place(1)
+        gate(0, 0, S)
+        place(2)
+        gate(1, 0, S)
+        gate(2, 0, S)
+        place(3)
+        gate(3, 0, HALF)
+        gate(3, HALF, S)
+
+        pages = [None] * PACK
+        for b in (1, 2, 3, 0):
+            pages[b] = tile(f"page{b}", [P, U], F32)
+            nc.gpsimd.memset(pages[b][:], 0.0)
+
+        z_codes = tile("z_codes", [P, S], U32)
+        z_plane = tile("z_plane", [P, S], U8)
+        for a in range(2):
+            cols = slice(HALF * a, HALF * (a + 1))
+            nc.vector.quantize_mx(
+                out=z_codes[:, cols].bitcast(FP8X4), scales=z_plane[:, cols], in_=z_bf[a][:].rearrange("p j t -> p (j t)")
+            )
+
+        def second(acc, b, cols):
+            nc.tensor.matmul_mx(
+                out=acc[:],
+                lhsT=d_codes[:, P * b : P * (b + 1)].bitcast(FP8X4),
+                lhsT_scale=d_plane[:, P * b : P * (b + 1)],
+                rhs=z_codes[:, cols].bitcast(FP8X4),
+                rhs_scale=z_plane[:, cols],
+                start=True,
+                stop=True,
+            )
+
+        pos = [tile(f"pos{b}", [P, S + 16], F32) for b in range(PACK)]
+        h_ps = [[] for b in range(PACK)]
+        for a in range(2):
+            cols = slice(HALF * a, HALF * (a + 1))
+            acc = psum.tile([P, HALF], F32, name=f"h_ps0{a}", tag="y_ps0" if a == 1 else "h_ps0")
+            second(acc, 0, cols)
+            nc.scalar.activation(pos[0][:, cols], acc[:], ACT.Relu, scale=0.0625)
+            h_ps[0].append((acc, cols))
+        for b in range(1, PACK):
+            acc = psum.tile([P, S], F32, name=f"h_ps{b}")
+            second(acc, b, slice(0, S))
+            nc.vector.tensor_scalar(pos[b][:, 0:S], acc[:], 0.0625, 0.0, ALU.mult, ALU.max)
+            h_ps[b].append((acc, slice(0, S)))
+
+        nw = [tile(f"nw{b}", [P, S], F32) for b in range(PACK)]
+
+        def fetch(b):
+            got = tile(f"got{b}", [P, S], F32)
+            nc.scalar.activation(got[:], pos[b][:].indirect(n4_t[:]), ACT.Copy)
+            for acc, cols in h_ps[b]:
+                nc.vector.scalar_tensor_tensor(nw[b][:, cols], acc[:], 0.0625, got[:, cols], ALU.mult, ALU.subtract)
+
+        def put(b):
+            nc.scalar.activation(pages[b][:].indirect(n3_t[:]), nw[b][:], ACT.Copy)
+            nc.sync.dma_start(out=out[P * b : P * (b + 1), :], in_=pages[b][:])
+
+        fetch(0)
+        fetch(1)
+        fetch(2)
+        put(0)
+        fetch(3)
+        put(1)
+        put(2)
+        put(3)

@@ -86,6 +86,11 @@ def tile_picked_hdenseerlpagez_none_p_kernel(
         nc.vector.memset(x_plane[:].bitcast(I32), 0)
         nc.vector.memset(d_plane[:].bitcast(I32), 0)
 
+        warm_in = tile("warm_in", [P, 1], F32)
+        warm_out = tile("warm_out", [P, 1], F32)
+        nc.vector.memset(warm_in[:], 0.0)
+        nc.scalar.activation(warm_out[:], warm_in[:], ACT.Sigmoid)
+
         xs_picked = tile("xs_picked", [P, S], U8)
         nc.vector.tensor_copy(xs_picked[:], xs_table[:].indirect(offs_t[:]))
         nc.sync.dma_start(

@@ -53,7 +53,7 @@ def tile_picked_hdenseerlpagez_none_p_kernel(
         xs_table = tile("xs_table", [P, T], U8, tag="scale_table")
         load_scale_table(nc.sync, xs_table, x_scales)
 
-        w1s_raw = tile("w1s_raw", [P, H], U8)
+        w1s_raw = tile("w1s_raw", [P, H], U8, tag="page1")
         w1s_rows = w1_scales[0].bitcast(I32).rearrange("(q r) c -> r q c", r=4)
         for r in range(4):
             nc.sync.dma_start(
@@ -81,7 +81,7 @@ def tile_picked_hdenseerlpagez_none_p_kernel(
         n4_t = load_list("n4_t", n4)
         n3_t = load_list("n3_t", n3)
 
-        x_plane = tile("x_plane", [P, S], U8, tag="page1")
+        x_plane = tile("x_plane", [P, S], U8)
         d_plane = tile("d_plane", [P, H], U8)
         nc.vector.memset(x_plane[:].bitcast(I32), 0)
         nc.vector.memset(d_plane[:].bitcast(I32), 0)
@@ -91,21 +91,28 @@ def tile_picked_hdenseerlpagez_none_p_kernel(
         nc.vector.memset(warm_in[:], 0.0)
         nc.scalar.activation(warm_out[:], warm_in[:], ACT.Sigmoid)
 
+        pages = [None] * PACK
+
+        def clear(b, tag):
+            pages[b] = tile(f"page{b}", [P, U], F32, tag=tag)
+            nc.vector.memset(pages[b][:].bitcast(I32), 0)
+
+        clear(0, "page0")
+
         xs_picked = tile("xs_picked", [P, S], U8)
         nc.vector.tensor_copy(xs_picked[:], xs_table[:].indirect(offs_t[:]))
         nc.sync.dma_start(
             out=x_plane[:].bitcast(I32)[0:PLANE_ROWS, :], in_=xs_picked[:].bitcast(I32)[SHIFT : SHIFT + PLANE_ROWS, :]
         )
 
-        w1_plane = tile("w1_plane", [P, H], U8, tag="page2")
+        w1_plane = tile("w1_plane", [P, H], U8)
         nc.vector.tensor_copy(
             w1_plane[:].rearrange("p (t m) -> p t m", t=PACK), w1s_raw[:].rearrange("p (m t) -> p t m", t=PACK)
         )
-        w1_codes = tile("w1_codes", [P, 2 * H], U8, tag="page3")
-        nc.scalar.copy(
-            w1_codes[:].bitcast(U16).rearrange("p (t m) -> p t m", t=PACK),
-            w1w_raw[:].bitcast(U16).rearrange("p (m t) -> p t m", t=PACK),
-        )
+        clear(1, "page1")
+        w1_codes = [tile(f"w1_codes{t}", [P, 2 * P], U8) for t in range(PACK)]
+        for t in range(PACK):
+            nc.scalar.copy(w1_codes[t][:].bitcast(U16), w1w_raw[:].bitcast(U16)[:, t:H:PACK])
         x_codes = tile("x_codes", [P, S], U32, tag="bytes")
         nc.vector.tensor_copy(x_codes[:], xw_table[:].bitcast(U32).indirect(offs_t[:]))
 
@@ -114,7 +121,7 @@ def tile_picked_hdenseerlpagez_none_p_kernel(
             acc = psum.tile([P, S], F32, name=f"y_ps{t}")
             nc.tensor.matmul_mx(
                 out=acc[:],
-                lhsT=w1_codes[:, 2 * P * t : 2 * P * (t + 1)].bitcast(FP4X4),
+                lhsT=w1_codes[t][:].bitcast(FP4X4),
                 lhsT_scale=w1_plane[:, P * t : P * (t + 1)],
                 rhs=x_codes[:].bitcast(FP8X4),
                 rhs_scale=x_plane[:],
@@ -123,7 +130,7 @@ def tile_picked_hdenseerlpagez_none_p_kernel(
             )
             y_ps.append(acc)
         for t in range(PACK):
-            y_sb.append(tile(f"y_sb{t}", [P, S], F32, tag="page0" if t == 0 else None))
+            y_sb.append(tile(f"y_sb{t}", [P, S], F32))
             nc.vector.tensor_copy(y_sb[t][:], y_ps[t][:])
 
 
@@ -173,11 +180,6 @@ def tile_picked_hdenseerlpagez_none_p_kernel(
         gate(3, 0, HALF)
         gate(3, HALF, S)
 
-        pages = [None] * PACK
-        for b in (1, 2, 3, 0):
-            pages[b] = tile(f"page{b}", [P, U], F32)
-            nc.gpsimd.memset(pages[b][:], 0.0)
-
         z_codes = tile("z_codes", [P, S], U32)
         z_plane = tile("z_plane", [P, S], U8)
         for a in range(2):
@@ -203,7 +205,10 @@ def tile_picked_hdenseerlpagez_none_p_kernel(
             cols = slice(HALF * a, HALF * (a + 1))
             acc = psum.tile([P, HALF], F32, name=f"h_ps0{a}", tag="y_ps0" if a == 1 else "h_ps0")
             second(acc, 0, cols)
-            nc.scalar.activation(pos[0][:, cols], acc[:], ACT.Relu, scale=0.0625)
+            if a == 0:
+                nc.scalar.activation(pos[0][:, cols], acc[:], ACT.Relu, scale=0.0625)
+            else:
+                nc.vector.tensor_scalar(pos[0][:, cols], acc[:], 0.0625, 0.0, ALU.mult, ALU.max)
             h_ps[0].append((acc, cols))
         for b in range(1, PACK):
             acc = psum.tile([P, S], F32, name=f"h_ps{b}")
@@ -228,6 +233,8 @@ def tile_picked_hdenseerlpagez_none_p_kernel(
         fetch(2)
         put(0)
         fetch(3)
+        clear(2, "pos0")
+        clear(3, "pos1")
         put(1)
         put(2)
         put(3)

from contextlib import ExitStack

import concourse.mybir as mybir

K, T, S, H, G, U = 512, 2048, 256, 512, 2048, 1024
FLOPS = 2 * K * H * S * 2

F32 = mybir.dt.float32
BF16 = mybir.dt.bfloat16
I32 = mybir.dt.int32
U32 = mybir.dt.uint32
U16 = mybir.dt.uint16
U8 = mybir.dt.uint8
FP8X4 = mybir.dt.float8_e4m3fn_x4
FP4X4 = mybir.dt.float4_e2m1fn_x4
ALU = mybir.AluOpType
ACT = mybir.ActivationFunctionType

P = 128
PACK = 4
SHIFT = 14
PLANE_ROWS = 100
ALIGN = 64
HALF = S // 2


def load_scale_table(queue, table, scales):
    rows = scales[0].bitcast(I32).rearrange("(a e) c -> e a c", e=2)
    words = table[:].bitcast(I32)
    for e in range(2):
        queue.dma_start(out=words[e:P:2, :], in_=rows[e].unsqueeze(1).to_broadcast([8, 8, rows.shape[2]]))


def tile_picked_hdenseerlpagez_none_p_kernel(
    tc, x_words, x_scales, w1_words, w1_scales, sl, th, gs, d_words, d_scales, offs, n1, n2, k1, n3, n4, out
):
    nc = tc.nc
    with ExitStack() as ctx:
        lists = ctx.enter_context(tc.tile_pool(name="lists", bufs=1))
        sb = ctx.enter_context(tc.tile_pool(name="sb", bufs=1))
        words = ctx.enter_context(tc.tile_pool(name="words", bufs=1))
        psum = ctx.enter_context(tc.psum_pool(name="psum", bufs=1))

        def load_list(name, src):
            tile = lists.tile(list(src.shape), U16, name=name)
            nc.sync.dma_start(tile[:], src)
            return tile

        def tile(name, shape, dtype, tag=None):
            return sb.tile(shape, dtype, name=name, tag=tag or name, align_bytes=ALIGN)

        offs_t = load_list("offs_t", offs)
        xs_table = tile("xs_table", [P, T], U8, tag="scale_table")
        load_scale_table(nc.sync, xs_table, x_scales)

        w1s_raw = tile("w1s_raw", [P, H], U8, tag="page1")
        w1s_rows = w1_scales[0].bitcast(I32).rearrange("(q r) c -> r q c", r=4)
        for r in range(4):
            nc.sync.dma_start(
                out=w1s_raw[:].bitcast(I32)[r:P:4, :], in_=w1s_rows[r].unsqueeze(1).to_broadcast([4, 8, H // 4])
            )
        w1w_raw = tile("w1w_raw", [P, 2 * H], U8)
        nc.gpsimd.dma_start(out=w1w_raw[:].bitcast(I32), in_=w1_words[0].bitcast(I32))

        xw_table = words.tile([P, T], I32, name="xw_table", align_bytes=ALIGN, offset=0)
        nc.sync.dma_start(out=xw_table[:], in_=x_words[0].rearrange("p c r -> p (c r)").bitcast(I32))

        n1_t = load_list("n1_t", n1)
        sl_t = tile("sl_t", [P, PACK], F32)
        th_t = tile("th_t", [P, PACK], F32)
        gs_t = tile("gs_t", [P, PACK], F32)
        nc.gpsimd.dma_start(out=sl_t[:], in_=sl.rearrange("(p t) o -> p (t o)", t=PACK))
        nc.gpsimd.dma_start(out=th_t[:], in_=th.rearrange("(p t) o -> p (t o)", t=PACK))
        sl_th = tile("sl_th", [P, PACK], F32)
        bias_t = tile("bias_t", [P, PACK], F32)
        nc.gpsimd.tensor_tensor(sl_th[:], sl_t[:], th_t[:], ALU.mult)
        nc.gpsimd.tensor_scalar(bias_t[:], sl_th[:], -1.0, 0.0, ALU.mult, ALU.add)
        n2_t = load_list("n2_t", n2)
        k1_t = load_list("k1_t", k1)
        nc.gpsimd.dma_start(out=gs_t[:], in_=gs.rearrange("(p t) o -> p (t o)", t=PACK))
        n4_t = load_list("n4_t", n4)
        n3_t = load_list("n3_t", n3)

        x_plane = tile("x_plane", [P, S], U8)
        d_plane = tile("d_plane", [P, H], U8)
        nc.vector.memset(x_plane[:].bitcast(I32), 0)
        nc.vector.memset(d_plane[:].bitcast(I32), 0)

        warm_in = tile("warm_in", [P, 1], F32)
        warm_out = tile("warm_out", [P, 1], F32)
        nc.vector.memset(warm_in[:], 0.0)
        nc.scalar.activation(warm_out[:], warm_in[:], ACT.Sigmoid)

        pages = [None] * PACK

        def clear(b, tag):
            pages[b] = tile(f"page{b}", [P, U], F32, tag=tag)
            nc.vector.memset(pages[b][:].bitcast(I32), 0)

        clear(0, "page0")

        xs_picked = tile("xs_picked", [P, S], U8)
        nc.vector.tensor_copy(xs_picked[:], xs_table[:].indirect(offs_t[:]))
        nc.sync.dma_start(
            out=x_plane[:].bitcast(I32)[0:PLANE_ROWS, :], in_=xs_picked[:].bitcast(I32)[SHIFT : SHIFT + PLANE_ROWS, :]
        )

        w1_plane = tile("w1_plane", [P, H], U8)
        nc.vector.tensor_copy(
            w1_plane[:].rearrange("p (t m) -> p t m", t=PACK), w1s_raw[:].rearrange("p (m t) -> p t m", t=PACK)
        )
        clear(1, "page1")
        w1_codes = [tile(f"w1_codes{t}", [P, 2 * P], U8) for t in range(PACK)]
        for t in range(PACK):
            nc.scalar.copy(w1_codes[t][:].bitcast(U16), w1w_raw[:].bitcast(U16)[:, t:H:PACK])
        x_codes = tile("x_codes", [P, S], U32, tag="bytes")
        nc.vector.tensor_copy(x_codes[:], xw_table[:].bitcast(U32).indirect(offs_t[:]))

        y_ps, y_sb = [], []
        for t in range(PACK):
            acc = psum.tile([P, S], F32, name=f"y_ps{t}")
            nc.tensor.matmul_mx(
                out=acc[:],
                lhsT=w1_codes[t][:].bitcast(FP4X4),
                lhsT_scale=w1_plane[:, P * t : P * (t + 1)],
                rhs=x_codes[:].bitcast(FP8X4),
                rhs_scale=x_plane[:],
                start=True,
                stop=True,
            )
            y_ps.append(acc)
        for t in range(PACK):
            y_sb.append(tile(f"y_sb{t}", [P, S], F32))
            nc.vector.tensor_copy(y_sb[t][:], y_ps[t][:])


        ds_table = tile("ds_table", [P, G], U8, tag="scale_table")
        load_scale_table(nc.sync, ds_table, d_scales)
        dw_table = words.tile([P, G], I32, name="dw_table", align_bytes=ALIGN, offset=0)
        nc.sync.dma_start(out=dw_table[:], in_=d_words[0].rearrange("p c r -> p (c r)").bitcast(I32))
        ds_picked = tile("ds_picked", [P, H], U8, tag="bytes")
        nc.vector.tensor_copy(ds_picked[:], ds_table[:].indirect(k1_t[:]))
        nc.sync.dma_start(
            out=d_plane[:].bitcast(I32)[0:PLANE_ROWS, :], in_=ds_picked[:].bitcast(I32)[SHIFT : SHIFT + PLANE_ROWS, :]
        )
        d_codes = tile("d_codes", [P, H], U32)
        nc.vector.tensor_copy(d_codes[:], dw_table[:].bitcast(U32).indirect(k1_t[:]))

        placed = [tile(f"placed{t}", [P, 2 * S], F32) for t in range(PACK)]
        z_bf = [
            words.tile([P, HALF, PACK], BF16, name=f"z_bf{a}", align_bytes=ALIGN, offset=a * HALF * PACK * 2)
            for a in range(2)
        ]
        sg = [tile(f"sg{t}", [P, S], F32) for t in range(PACK)]

        def place(t):
            nc.scalar.activation(placed[t][:].indirect(n1_t[:]), y_sb[t][:], ACT.Copy)

        def gate(t, lo, hi):
            nc.scalar.activation(
                sg[t][:, lo:hi],
                placed[t][:].indirect(n2_t[:, lo // 16 : hi // 16]),
                ACT.Sigmoid,
                bias=bias_t[:, t : t + 1],
                scale=sl_t[:, t : t + 1],
            )
            for a in range(lo // HALF, hi // HALF):
                cols = slice(HALF * a, HALF * (a + 1))
                nc.vector.scalar_tensor_tensor(
                    z_bf[a][:, :, t], y_ps[t][:, cols], gs_t[:, t : t + 1], sg[t][:, cols], ALU.mult, ALU.mult
                )

        place(0)
        place(1)
        gate(0, 0, S)
        place(2)
        gate(1, 0, S)
        gate(2, 0, S)
        place(3)
        gate(3, 0, HALF)
        gate(3, HALF, S)

        z_codes = tile("z_codes", [P, S], U32)
        z_plane = tile("z_plane", [P, S], U8)
        for a in range(2):
            cols = slice(HALF * a, HALF * (a + 1))
            nc.vector.quantize_mx(
                out=z_codes[:, cols].bitcast(FP8X4), scales=z_plane[:, cols], in_=z_bf[a][:].rearrange("p j t -> p (j t)")
            )

        def second(acc, b, cols):
            nc.tensor.matmul_mx(
                out=acc[:],
                lhsT=d_codes[:, P * b : P * (b + 1)].bitcast(FP8X4),
                lhsT_scale=d_plane[:, P * b : P * (b + 1)],
                rhs=z_codes[:, cols].bitcast(FP8X4),
                rhs_scale=z_plane[:, cols],
                start=True,
                stop=True,
            )

        pos = [tile(f"pos{b}", [P, S + 16], F32) for b in range(PACK)]
        h_ps = [[] for b in range(PACK)]
        for a in range(2):
            cols = slice(HALF * a, HALF * (a + 1))
            acc = psum.tile([P, HALF], F32, name=f"h_ps0{a}", tag="y_ps0" if a == 1 else "h_ps0")
            second(acc, 0, cols)
            if a == 0:
                nc.scalar.activation(pos[0][:, cols], acc[:], ACT.Relu, scale=0.0625)
            else:
                nc.vector.tensor_scalar(pos[0][:, cols], acc[:], 0.0625, 0.0, ALU.mult, ALU.max)
            h_ps[0].append((acc, cols))
        for b in range(1, PACK):
            acc = psum.tile([P, S], F32, name=f"h_ps{b}")
            second(acc, b, slice(0, S))
            nc.vector.tensor_scalar(pos[b][:, 0:S], acc[:], 0.0625, 0.0, ALU.mult, ALU.max)
            h_ps[b].append((acc, slice(0, S)))

        nw = [tile(f"nw{b}", [P, S], F32) for b in range(PACK)]

        def fetch(b):
            got = tile(f"got{b}", [P, S], F32)
            nc.scalar.activation(got[:], pos[b][:].indirect(n4_t[:]), ACT.Copy)
            for acc, cols in h_ps[b]:
                nc.vector.scalar_tensor_tensor(nw[b][:, cols], acc[:], 0.0625, got[:, cols], ALU.mult, ALU.subtract)

        def put(b):
            nc.scalar.activation(pages[b][:].indirect(n3_t[:]), nw[b][:], ACT.Copy)
            nc.sync.dma_start(out=out[P * b : P * (b + 1), :], in_=pages[b][:])

        fetch(0)
        fetch(1)
        fetch(2)
        put(0)
        fetch(3)
        clear(2, "pos0")
        clear(3, "pos1")
        put(1)
        put(2)
        put(3)
